import numpy as np
import ml_dtypes


def mxq(x, axis, fmt="e4m3"):
    dtype, down = {"e4m3": (ml_dtypes.float8_e4m3fn, 7), "e5m2": (ml_dtypes.float8_e5m2, 14)}[fmt]
    v = np.moveaxis(np.asarray(x, np.float32).astype(ml_dtypes.bfloat16).astype(np.float64), axis, -1)
    blocks = v.reshape(v.shape[:-1] + (-1, 32))
    amax = np.abs(blocks).max(-1, keepdims=True)
    byte = np.maximum(np.where(amax > 0, np.frexp(amax)[1] - 1 + 127, 0) - down, 1)
    scale = np.exp2(byte - 127.0)
    codes = (blocks / scale).astype(np.float32).astype(dtype).astype(np.float64)
    return np.moveaxis((codes * scale).reshape(v.shape), -1, axis)


WIDE = False


def mx_kscale(k):
    if not WIDE:
        return np.ones(k)
    levels = np.array([10, -10, 5, -5, 0])
    if k % 512:
        return np.exp2(np.random.permutation(np.resize(levels, k // 32))).repeat(32)
    a = np.empty((k // 512, 16))
    for p in range(k // 512):
        a[p, :8] = np.random.permutation(np.resize(levels, 8))
        for g in range(8):
            far = levels[np.abs(levels - a[p, g]) >= 10]
            a[p, g + 8] = far[np.random.randint(len(far))]
    return np.exp2(a.ravel()).repeat(32)


def f64(x):
    return np.asarray(x).astype(np.float64)


def striped(idx):
    return np.tile(idx.reshape(-1, 16).T, (8, 1)).astype(np.uint16)


def unstriped(offs):
    return offs[:16].T.reshape(-1).astype(np.int64)


def striped8(idx):
    return np.concatenate([x.reshape(-1, 16).T for x in idx]).astype(np.uint16)


def runs(offs, k):
    lists = np.stack([offs[16 * r : 16 * r + 16].T.reshape(-1) for r in range(8)]).astype(np.int64)
    return lists[np.arange(k) % 512 // 64]


def pack_weight(w):
    k, n = w.shape
    w = f64(np.asarray(w, np.float32).astype(ml_dtypes.bfloat16)).reshape(k // 32, 32, n)
    amax = np.abs(w).max(1)
    byte = np.clip(np.where(amax > 0, np.frexp(amax)[1] - 1 + 127 - 7, 1), 1, 254)
    scaled = (w * np.exp2(127.0 - byte)[:, None, :]).reshape(k, n).astype(np.float32)
    words = np.ascontiguousarray(scaled.reshape(k // 512, 128, 4, n).transpose(0, 1, 3, 2)).astype(ml_dtypes.float8_e4m3fn).view(np.uint8)
    return words, np.ascontiguousarray(byte.astype(np.uint8).reshape(k // 512, 16, n))


def unpack_weight(words, scales):
    g, p, n, _ = words.shape
    vals = np.ascontiguousarray(words).view(ml_dtypes.float8_e4m3fn).astype(np.float64) * np.repeat(np.exp2(scales.astype(np.float64) - 127.0), 8, axis=1)[..., None]
    return vals.transpose(0, 1, 3, 2).reshape(g * 512, n)


E2M1 = np.array([0.0, 0.5, 1.0, 1.5, 2.0, 3.0, 4.0, 6.0, -0.0, -0.5, -1.0, -1.5, -2.0, -3.0, -4.0, -6.0])


def pack_fp4(w):
    k, n = w.shape
    w = f64(np.asarray(w, np.float32).astype(ml_dtypes.bfloat16)).reshape(k // 32, 32, n)
    amax = np.abs(w).max(1)
    mant, ex = np.frexp(amax / 6.0)
    byte = np.clip(np.where(amax > 0, np.where(mant > 0.5, ex, ex - 1) + 127, 1), 1, 254)
    scaled = (w * np.exp2(127.0 - byte)[:, None, :]).reshape(k, n).astype(np.float32)
    c = np.ascontiguousarray(scaled.reshape(k // 512, 128, 4, n).transpose(0, 1, 3, 2)).astype(ml_dtypes.float4_e2m1fn).view(np.uint8) & 0xF
    words = (c[..., 0::2] | (c[..., 1::2] << 4)).reshape(k // 512, 128, 2 * n)
    return np.ascontiguousarray(words), np.ascontiguousarray(byte.astype(np.uint8).reshape(k // 512, 16, n))


def unpack_fp4(words, scales):
    g, _, n = scales.shape
    words = np.ascontiguousarray(words).reshape(g, 128, n, 2)
    nib = np.empty((g, 128, n, 4), np.uint8)
    nib[..., 0::2] = words & 0xF
    nib[..., 1::2] = words >> 4
    vals = E2M1[nib] * np.repeat(np.exp2(scales.astype(np.float64) - 127.0), 8, axis=1)[..., None]
    return vals.transpose(0, 1, 3, 2).reshape(g * 512, n)


def sigmoid(v):
    return 1.0 / (1.0 + np.exp(-np.maximum(v, -700.0)))

def planes(y):
    n, m = y.shape
    v = y.astype(np.float32).astype(ml_dtypes.bfloat16).astype(np.float64).reshape(n // 32, 32, m)
    top = np.abs(v).max(1)
    byte = np.clip(np.where(top > 0, np.frexp(top)[1] - 1 + 127 - 7, 1), 1, 254)
    codes = (v * np.exp2(127.0 - byte)[:, None, :]).reshape(n, m).astype(np.float32).astype(ml_dtypes.float8_e4m3fn).view(np.uint8)
    words = codes.reshape(n // 512, 128, 4, m).transpose(0, 1, 3, 2)
    return np.ascontiguousarray(words), np.ascontiguousarray(byte.astype(np.uint8).reshape(n // 512, 16, m))


K, T, S, N, H = 512, 2048, 512, 512, 512


def setup_inputs():
    n = np.random.standard_normal
    s = mx_kscale(K)[:, None]
    u = mx_kscale(H)
    packed_xT = pack_weight(n((K, T)) * s)
    packed_w1 = pack_fp4(n((K, H)) / np.sqrt(K) / s)
    packed_w2 = pack_fp4(n((H, N)) / np.sqrt(H) / u[:, None])
    packed_w3 = pack_fp4(n((K, N)) / np.sqrt(K) / s)
    return {
        "x_words": packed_xT[0],
        "x_scales": packed_xT[1],
        "w1_words": packed_w1[0],
        "w1_scales": packed_w1[1],
        "gn": (np.random.uniform(0.5, 1.5, (H, 1)) * u[:, None]).astype(np.float32),
        "w2_words": packed_w2[0],
        "w2_scales": packed_w2[1],
        "w3_words": packed_w3[0],
        "w3_scales": packed_w3[1],
        "offs": striped(np.random.permutation(T)[:S]),
        "n1": striped8(np.stack([np.random.permutation(S) for _ in range(8)])),
        "n2": striped8(np.stack([np.random.permutation(S) for _ in range(8)])),
        "two": striped(np.random.permutation(T)[:S]),
        "n3": striped8(np.stack([np.random.permutation(S) for _ in range(8)])),
        "n4": striped8(np.stack([np.random.permutation(S) for _ in range(8)])),
    }


def reference(x_words, x_scales, w1_words, w1_scales, gn, w2_words, w2_scales, w3_words, w3_scales, offs, n1, n2, two, n3, n4):
    xq = unpack_weight(x_words, x_scales)[:, unstriped(offs)]
    y = unpack_fp4(w1_words, w1_scales).T @ xq
    st = y + y[np.arange(H)[:, None], runs(n1, H)]
    z = f64(gn) * (st * (np.tanh(st[np.arange(H)[:, None], runs(n2, H)])))
    h = unpack_fp4(w2_words, w2_scales).T @ mxq(z, 0, "e4m3")
    x_two = unpack_weight(x_words, x_scales)[:, unstriped(two)]
    d = unpack_fp4(w3_words, w3_scales).T @ x_two
    out_0 = h + (sigmoid(d[np.arange(N)[:, None], runs(n4, N)] - d)) * (h[np.arange(N)[:, None], runs(n3, N)] - h)
    return (out_0,) + planes(out_0)

from contextlib import ExitStack

import concourse.mybir as mybir

K, T, S, H, N = 512, 2048, 512, 512, 512
FLOPS = 3 * 2 * K * S * N

F32 = mybir.dt.float32
BF16 = mybir.dt.bfloat16
I32 = mybir.dt.int32
U32 = mybir.dt.uint32
U16 = mybir.dt.uint16
U8 = mybir.dt.uint8
FP8X4 = mybir.dt.float8_e4m3fn_x4
FP4X4 = mybir.dt.float4_e2m1fn_x4
ACT = mybir.ActivationFunctionType
ALU = mybir.AluOpType

P = 128
PACK = 4
HALF = S // 2
OUT_CHUNKS = ((0, 256), (256, 128), (384, 128))


def tile_picked_latepullbhopp_none_po_kernel(
    tc, x_words, x_scales, w1_words, w1_scales, gn, w2_words, w2_scales, w3_words, w3_scales,
    offs, n1, n2, two, n3, n4, out_0, out_1, out_2,
):
    nc = tc.nc
    with ExitStack() as ctx:
        lists = ctx.enter_context(tc.tile_pool(name="lists", bufs=1))
        sb = ctx.enter_context(tc.tile_pool(name="sb", bufs=1))
        psum = ctx.enter_context(tc.psum_pool(name="psum", bufs=1))

        def load_list(src, name):
            tile = lists.tile([P, S // 16], U16, name=name)
            nc.sync.dma_start(tile[:], src)
            return tile

        def load_scale_rows(queues, dst, src):
            for q in range(4):
                queues[q].dma_start(dst[32 * q : 32 * q + 4, :].bitcast(I32), src[0, 4 * q : 4 * q + 4, :].bitcast(I32))

        def load_words(queue, src):
            tile = sb.tile([P, 2 * N], U8, name="raw_words")
            queue.dma_start(tile[:].bitcast(I32), src[0].bitcast(I32))
            return tile

        def deal_words(raw, name):
            dealt = sb.tile([P, 2 * N], U8, name=name, align_bytes=64)
            nc.vector.tensor_copy(
                out=dealt[:].rearrange("p (t m b) -> p t m b", t=PACK, b=2),
                in_=raw[:].rearrange("p (m t b) -> p t m b", t=PACK, b=2),
            )
            return dealt

        def deal_scales(raw, name):
            dealt = sb.tile([P, N], U8, name=name, align_bytes=64)
            nc.vector.tensor_copy(
                out=dealt[:].rearrange("p (t m) -> p t m", t=PACK),
                in_=raw[:].rearrange("p (m t) -> p t m", t=PACK),
            )
            return dealt

        def product(bank, words, scales, t, codes, code_scales):
            nc.tensor.matmul_mx(
                out=bank,
                lhsT=words[:, 2 * P * t : 2 * P * (t + 1)].bitcast(FP4X4),
                lhsT_scale=scales[:, P * t : P * (t + 1)],
                rhs=codes.bitcast(FP8X4),
                rhs_scale=code_scales,
                start=True,
                stop=True,
            )

        def look_up(out, window, offsets, first, width, other, op):
            nc.vector.tensor_tensor(
                out, window[:].indirect(offsets[:, first // 16 : (first + width) // 16]), other, op
            )

        def interleave(copy, dst, src):
            copy(
                out=dst.rearrange("p (c i t) -> p c t i", t=PACK, i=4),
                in_=src.rearrange("p t (c i) -> p c t i", i=4),
            )

        xs = sb.tile([P, T], U8, name="xs")
        nc.gpsimd.memset(xs[:].bitcast(I32), 0)
        raw_scales = sb.tile([P, N], U8, name="raw_scales")
        nc.vector.memset(raw_scales[:].bitcast(I32), 0)
        warm_in = sb.tile([P, 1], F32, name="warm_in")
        warm_out = sb.tile([P, 1], F32, name="warm_out")
        nc.vector.memset(warm_in[:], 0.0)

        offs_t = load_list(offs, "offs_t")
        w1_raw = load_words(nc.sync, w1_words)
        xw = sb.tile([P, T], I32, name="xw")
        nc.sync.dma_start(xw[:], x_words[0].rearrange("p n r -> p (n r)").bitcast(I32))
        load_scale_rows([nc.scalar] * 4, xs, x_scales)
        load_scale_rows([nc.scalar, nc.scalar, nc.gpsimd, nc.gpsimd], raw_scales, w1_scales)
        nc.scalar.activation(warm_out[:], warm_in[:], ACT.Sigmoid)
        two_t = load_list(two, "two_t")
        n1_t = load_list(n1, "n1_t")
        gain = sb.tile([P, PACK], F32, name="gain")
        nc.sync.dma_start(gain[:], gn.rearrange("(p t) o -> p (t o)", t=PACK))
        n2_t = load_list(n2, "n2_t")
        n4_t = load_list(n4, "n4_t")
        n3_t = load_list(n3, "n3_t")

        def pick_scales(offsets, name):
            picked = sb.tile([P, S], U8, name=name, align_bytes=64)
            nc.vector.tensor_copy(picked[:], xs[:].indirect(offsets[:]))
            return picked

        def pick_words(offsets, name):
            picked = sb.tile([P, S], U32, name=name, align_bytes=64)
            nc.vector.tensor_copy(picked[:], xw[:].bitcast(U32).indirect(offsets[:]))
            return picked

        w1 = deal_words(w1_raw, "w1")
        xa_scales = pick_scales(offs_t, "xa_scales")
        w1s = deal_scales(raw_scales, "w1s")
        w3_raw = load_words(nc.sync, w3_words)
        load_scale_rows([nc.sync] * 4, raw_scales, w3_scales)
        xa = pick_words(offs_t, "xa")
        xb_scales = pick_scales(two_t, "xb_scales")
        xb = pick_words(two_t, "xb")
        w3 = deal_words(w3_raw, "w3")
        w3s = deal_scales(raw_scales, "w3s")
        w2_raw = load_words(nc.sync, w2_words)
        load_scale_rows([nc.sync] * 4, raw_scales, w2_scales)

        y_banks = [psum.tile([P, S], F32, name="y_bank%d" % t, tag="a%d" % t) for t in range(PACK)]
        d_banks = [psum.tile([P, S], F32, name="d_bank%d" % t, tag="b%d" % t) for t in range(PACK)]
        for t in range(PACK):
            product(y_banks[t][:], w1, w1s, t, xa[:], xa_scales[:])
        for t in range(PACK):
            product(d_banks[t][:], w3, w3s, t, xb[:], xb_scales[:])

        def leave_bank(bank, name):
            window = sb.tile([P, S], F32, name=name + "_window")
            plain = sb.tile([P, S], F32, name=name + "_plain")
            nc.scalar.copy(window[:], bank[:])
            nc.scalar.copy(plain[:], bank[:])
            return window, plain

        st = []
        for t in range(PACK):
            window, plain = leave_bank(y_banks[t], "y%d" % t)
            tile = sb.tile([P, S], F32, name="st%d" % t)
            for a in (0, HALF):
                look_up(tile[:, a : a + HALF], window, n1_t, a, HALF, plain[:, a : a + HALF], ALU.add)
            st.append(tile)

        w2 = deal_words(w2_raw, "w2")
        w2s = deal_scales(raw_scales, "w2s")

        z = [sb.tile([P, PACK, HALF], F32, name="z%d" % c) for c in range(2)]
        for t in range(PACK):
            tanh = sb.tile([P, S], F32, name="tanh%d" % t)
            gained = sb.tile([P, S], F32, name="gained%d" % t)
            nc.scalar.activation(tanh[:], st[t][:], ACT.Tanh)
            nc.scalar.activation(gained[:], st[t][:], ACT.Copy, scale=gain[:, t : t + 1])
            for c in range(2):
                a = c * HALF
                look_up(z[c][:, t, :], tanh, n2_t, a, HALF, gained[:, a : a + HALF], ALU.mult)

        z_codes = [sb.tile([P, HALF], U32, name="z_codes%d" % c, align_bytes=64) for c in range(2)]
        z_scales = [sb.tile([P, HALF], U8, name="z_scales%d" % c, align_bytes=64) for c in range(2)]
        z_rounded = [sb.tile([P, PACK * HALF], BF16, name="z_rounded%d" % c, align_bytes=64) for c in range(2)]
        for c in range(2):
            interleave(nc.vector.tensor_copy, z_rounded[c][:], z[c][:])
        for c in range(2):
            nc.vector.quantize_mx(out=z_codes[c][:].bitcast(FP8X4), scales=z_scales[c][:], in_=z_rounded[c][:])

        h_banks = [psum.tile([P, S], F32, name="h_bank%d" % t, tag="a%d" % t) for t in range(PACK)]
        for t in range(PACK):
            for c in range(2):
                product(h_banks[t][:, c * HALF : (c + 1) * HALF], w2, w2s, t, z_codes[c][:], z_scales[c][:])

        pulls = []
        for t in range(PACK):
            window, plain = leave_bank(d_banks[t], "d%d" % t)
            tile = sb.tile([P, S], F32, name="pull%d" % t)
            for a in (0, HALF):
                look_up(tile[:, a : a + HALF], window, n4_t, a, HALF, plain[:, a : a + HALF], ALU.subtract)
            pulls.append(tile)

        h_plain = sb.tile([P, PACK, S], F32, name="h_plain")
        h_windows = []
        for t in range(PACK):
            window = sb.tile([P, S], F32, name="h%d_window" % t)
            nc.scalar.copy(window[:], h_banks[t][:])
            nc.scalar.copy(h_plain[:, t, :], h_banks[t][:])
            h_windows.append(window)

        gate = sb.tile([P, PACK, S], F32, name="gate")
        for t in range(PACK):
            nc.scalar.activation(gate[:, t, :], pulls[t][:], ACT.Sigmoid)

        out_codes = sb.tile([P, S], I32, name="out_codes", align_bytes=64)
        out_scales = sb.tile([P, S], U8, name="out_scales", align_bytes=64)
        out_rows = out_0.rearrange("(p t) n -> p t n", t=PACK)
        out_words = out_1[0].rearrange("p n r -> p (n r)").bitcast(I32)
        for c, (a, width) in enumerate(OUT_CHUNKS):
            cols = slice(a, a + width)
            step = sb.tile([P, PACK, width], F32, name="step%d" % c)
            gated = sb.tile([P, PACK, width], F32, name="gated%d" % c)
            result = sb.tile([P, PACK, width], F32, name="result%d" % c)
            rounded = sb.tile([P, PACK * width], BF16, name="rounded%d" % c, align_bytes=64)
            for t in range(PACK):
                look_up(step[:, t, :], h_windows[t], n3_t, a, width, h_plain[:, t, cols], ALU.subtract)
            nc.vector.tensor_tensor(gated[:], step[:], gate[:, :, cols], ALU.mult)
            nc.vector.tensor_tensor(result[:], gated[:], h_plain[:, :, cols], ALU.add)
            nc.sync.dma_start(out_rows[:, :, cols], result[:])
            last = c == len(OUT_CHUNKS) - 1
            interleave(nc.vector.tensor_copy if last else nc.scalar.copy, rounded[:], result[:])
            nc.vector.quantize_mx(out=out_codes[:, cols].bitcast(FP8X4), scales=out_scales[:, cols], in_=rounded[:])
            nc.sync.dma_start(out_words[:, cols], out_codes[:, cols])
        for q in range(4):
            queue = nc.sync if q % 2 == 0 else nc.scalar
            queue.dma_start(out_2[0, 4 * q : 4 * q + 4, :].bitcast(I32), out_scales[32 * q : 32 * q + 4, :].bitcast(I32))
